import numpy as np, ml_dtypes
CORES = [51,54,179,182]
N = 4
import mx_ref
NC, KT = 256, 1
OWNER = [2,3,3,3]
BF = ml_dtypes.bfloat16
def setup_inputs(rng):
    def f(*shape):
        return mx_ref.flush((rng.standard_normal(shape, dtype=np.float32) * np.exp2(rng.integers(-2, 3, shape[:-1] + (1,)))).astype(BF))
    return {"w": f(N, 128, KT * 512), "x": f(N, 128, KT * 4 * NC)}
def setup_inputs_blocks(rng):
    d = setup_inputs(rng)
    for k in ("w", "x"): d[k] = mx_ref.spread(d[k], rng, 4)
    return d
def setup_inputs_wide(rng):
    d = setup_inputs(rng)
    for k in ("w", "x"): d[k] = mx_ref.flush((d[k].astype(np.float32) * np.exp2(rng.integers(-8, 9, (N, 1, 1))).astype(np.float32)).astype(BF))
    return d
def setup_inputs_zeros(rng):
    d = setup_inputs(rng); v = d["x"].reshape(N, 128, -1, 4).copy()
    v[np.broadcast_to((rng.random((N, 1, v.shape[2], 1)) < 0.33), v.shape)] = 0
    d["x"] = v.reshape(d["x"].shape)
    return d
def reference(w, x):
    y = np.zeros((N, 128, NC), np.float32)
    for r in range(N):
        for t in range(KT):
            p = mx_ref.matmul(mx_ref.quantize(w[OWNER[r]][:, 512 * t:512 * t + 512]), mx_ref.quantize(x[r][:, 4 * NC * t:4 * NC * t + 4 * NC]))
            y[r] = p if t == 0 else y[r] + p
    return {"y": y}

from concourse.bass import DstId, RemoteDMATransfer
from concourse.mybir import dt, ActivationFunctionType

ENGINES = 4
HALF = 128

SCRATCH = {
    "wb": ("sbuf", [128, 512], "bfloat16"),
    "xb": ("sbuf", [128, 1024], "bfloat16"),
    "wq": ("sbuf", [128, 128], "float8_e4m3fn_x4"),
    "ws": ("sbuf", [128, 128], "uint8"),
    "xq": ("sbuf", [128, 256], "float8_e4m3fn_x4"),
    "xs": ("sbuf", [128, 256], "uint8"),
    "lq": ("sbuf", [128, 128], "float8_e4m3fn_x4"),
    "ls": ("sbuf", [128, 128], "uint8"),
    "ps": ("psum", [128, 1024], "float32"),
    "yb": ("sbuf", [128, 256], "float32"),
}
SEMAPHORES = ["wl", "xl", "wp", "xp", "arr", "sent", "m0", "m1", "cp", "st"]


def _bits(mask):
    return [b for b in range(mask.bit_length()) if (mask >> b) & 1]


def _masks(core, dests, topo):
    out, narrow, taken = {}, 0, 0
    for d in sorted(dests, key=lambda d: len(_bits(topo.mask(core, d)))):
        allowed = topo.mask(core, d)
        free = _bits(allowed & ~narrow)
        if len(free) < ENGINES:
            free = _bits(allowed & ~taken)
        m = 0
        for b in free[::len(free) // ENGINES][:ENGINES]:
            m |= 1 << b
        out[d] = m
        taken |= m
        narrow |= allowed
    return out


def rank_program(g, core, T, topo):
    rank = T.rank_of(core)
    if rank is None:
        return
    owner, S = T.tables["OWNER"], T.sem
    users = [r for r in range(len(owner)) if owner[r] == rank]
    dests = [T.cores[r] for r in users if r != rank]
    own = owner[rank] == rank

    if users:
        g.sync.dma_start(T.wb[:], T.w[:]).then_inc(S.wl, 16)
    g.sync.dma_start(T.xb[:], T.x[:]).then_inc(S.xl, 16)

    if users:
        g.vector.wait_ge(S.wl, 16)
        g.vector.quantize_mx(T.wq[:], T.ws[:], T.wb[:]).then_inc(S.wp, 1)
    g.vector.wait_ge(S.xl, 16)
    g.vector.quantize_mx(T.xq[:], T.xs[:], T.xb[:]).then_inc(S.xp, 1)

    if dests:
        masks = _masks(core, dests, topo)
        g.wait_ge(S.wp, 1)
        for src, dst in ((T.wq[:].bitcast(dt.uint8), T.lq[:].bitcast(dt.uint8)), (T.ws[:], T.ls[:])):
            transfers = []
            for d in dests:
                rid, pid = topo.addr(d, core)
                transfers.append(RemoteDMATransfer(dst_ids=[DstId(rid=rid, pnc=pid)], dma_engine_mask=masks[d],
                                                   remote_sem=S.arr, src=src, dst=dst))
            g.remote_dma_fused(transfers, local_sem=S.sent)

    g.tensor.wait_ge(S.xp, 1)
    if own:
        g.tensor.wait_ge(S.wp, 1)
        a, a_s = T.wq, T.ws
    else:
        g.tensor.wait_ge(S.arr, 2 * ENGINES)
        a, a_s = T.lq, T.ls
    g.tensor.matmul_mx(T.ps[:, 0:HALF], a[:], a_s[:], T.xq[:, 0:HALF], T.xs[:, 0:HALF], True, True).then_inc(S.m0, 1)
    g.tensor.matmul_mx(T.ps[:, 512:512 + HALF], a[:], a_s[:], T.xq[:, HALF:2 * HALF], T.xs[:, HALF:2 * HALF],
                       True, True).then_inc(S.m1, 1)

    g.vector.wait_ge(S.m0, 1)
    g.vector.tensor_copy(T.yb[:, 0:HALF], T.ps[:, 0:HALF]).then_inc(S.cp, 1)
    g.scalar.wait_ge(S.m1, 1)
    g.scalar.activation(T.yb[:, HALF:2 * HALF], T.ps[:, 512:512 + HALF], ActivationFunctionType.Copy).then_inc(S.cp, 1)
    g.sync.wait_ge(S.cp, 2)
    g.sync.dma_start(T.y[:], T.yb[:]).then_inc(S.st, 16)
    g.sync.wait_ge(S.st, 16)

    if dests:
        g.wait_ge(S.sent, 2 * ENGINES * len(dests))
